import numpy as np
CORES = [2,3,10,11,18,19,26,27,34,35,42,43,50,51,58,59]
N = 16
def setup_inputs(rng):
    return {"x": rng.standard_normal((N, 128, 256), dtype=np.float32)}
def reference(x):
    s = (x.sum(axis=0, dtype=np.float64) / N).astype(x.dtype)
    b = 256 // N
    return {"y": np.stack([s[:, r * b:(r + 1) * b] for r in range(N)])}

from concourse.bass import DstId, RemoteDMATransfer
from concourse.mybir import AluOpType

SCRATCH = {
    "xs": ("sbuf", [128, 2, 2, 2, 2, 16], "float32"),
    "xp": ("sbuf", [128, 2, 2, 2, 2, 16], "float32"),
    "k16": ("sbuf", [128, 2, 2, 16], "float32"),
    "landA": ("sbuf", [128, 2, 2, 2, 16], "float32"),
    "landB": ("sbuf", [128, 2, 16], "float32"),
    "landC": ("sbuf", [128, 4, 16], "float32"),
    "tmp": ("sbuf", [128, 16], "float32"),
    "half": ("sbuf", [128, 2, 16], "float32"),
    "out": ("sbuf", [128, 16], "float32"),
}
SEMAPHORES = ["ld", "kset", "perm", "arrA", "arrB", "arrC", "sent", "pre1", "pre2", "sum1", "fin", "st"]


def _place(core):
    k, j = divmod(core, 8)
    if j not in (2, 3, 6, 7):
        return None
    P, Q = divmod(k, 2)
    H, PL = divmod(P, 2)
    return k, P, Q, H, PL, (0 if j < 4 else 1), (H if j in (2, 6) else 1 - H)


def _worker(k, c, h):
    return 8 * k + (2 if c == 0 else 6) + (0 if h == (k // 4) else 1)


def _c_sends(core):
    k, P, Q, H, PL, c, h = _place(core)
    dsts = [(8 * (2 * (2 * h + pl) + Q) + 2 + c, pl) for pl in (0, 1)]
    dsts = [d for d in dsts if d[0] != core]
    if len(dsts) == 1:
        return [(dsts[0][0], dsts[0][1], 0xFF, 8)]
    return [(dsts[0][0], dsts[0][1], 0x0F, 4), (dsts[1][0], dsts[1][1], 0xF0, 4)]


def rank_program(g, core, T, topo):
    place = _place(core)
    if place is None:
        return
    k, P, Q, H, PL, c, h = place
    S = T.sem
    rank = T.rank_of(core)
    add = AluOpType.add

    def dst_id(d):
        rid, pid, _ = topo.addr(d)
        return DstId(rid=rid, pnc=pid)

    def piece(copy, *idx):
        return copy[0][(slice(None),) + copy[1] + idx]

    sent = 0
    if rank is not None:
        me = rank % 2
        g.sync.dma_start(T.xs[:], T.x[:]).then_inc(S.ld, 16)
        g.vector.memset(T.k16[:], 0.0625).then_inc(S.kset, 1)
        g.vector.wait_ge(S.kset, 1)
        g.vector.wait_ge(S.ld, 16)
        for cc in (0, 1):
            for q in (0, 1):
                g.vector.tensor_tensor(T.xp[:, cc, :, q, :, :], T.xs[:, :, :, q, cc, :], T.k16[:],
                                       AluOpType.mult).then_inc(S.perm, 1)
        g.wait_ge(S.perm, 4)
        tr = []
        for cc in (0, 1):
            for hh in (0, 1):
                w = _worker(k, cc, hh)
                if w != core:
                    tr.append(RemoteDMATransfer(dst_ids=[dst_id(w)], dma_engine_mask=0xF << (4 * len(tr)),
                                                remote_sem=S.arrA, src=T.xp[:, cc, hh], dst=T.landA[:, me]))
        g.remote_dma_fused(tr, local_sem=S.sent)
        sent += 12
        copies = [(T.xp, (c, h)), (T.landA, (1 - me,))]
        n_a = 4
    else:
        copies = [(T.landA, (0,)), (T.landA, (1,))]
        n_a = 8

    g.wait_ge(S.arrA, n_a)
    g.remote_dma_fused([RemoteDMATransfer(dst_ids=[dst_id(core ^ 8)], dma_engine_mask=0xFF, remote_sem=S.arrB,
                                          srcs=[piece(a, 1 - Q) for a in copies], dsts=[T.landB[:]], alu_op=1)],
                       local_sem=S.sent)
    sent += 8

    g.wait_ge(S.arrB, 8)
    g.remote_dma_fused([RemoteDMATransfer(dst_ids=[dst_id(d)], dma_engine_mask=m, remote_sem=S.arrC,
                                          srcs=[piece(a, Q, pl) for a in copies] + [T.landB[:, pl]],
                                          dsts=[T.landC[:, P]], alu_op=1)
                        for d, pl, m, n in _c_sends(core)], local_sem=S.sent)
    sent += 8

    if rank is not None:
        v = g.vector
        if c == 0 and h == H:
            v.wait_ge(S.perm, 4)
            v.wait_ge(S.arrA, n_a)
            v.tensor_tensor(T.tmp[:], piece(copies[0], Q, PL), piece(copies[1], Q, PL), add).then_inc(S.pre1, 1)
            v.wait_ge(S.pre1, 1)
            v.wait_ge(S.arrB, 8)
            v.tensor_tensor(T.landC[:, P], T.tmp[:], T.landB[:, PL], add).then_inc(S.pre2, 1)
            v.wait_ge(S.pre2, 1)
        n_c = 0
        for kk in range(8):
            for j in (2, 3, 6, 7):
                n_c += sum(n for d, pl, m, n in _c_sends(8 * kk + j) if d == core)
        v.wait_ge(S.arrC, n_c)
        v.tensor_tensor(T.half[:], T.landC[:, 0:2], T.landC[:, 2:4], add).then_inc(S.sum1, 1)
        v.wait_ge(S.sum1, 1)
        v.tensor_tensor(T.out[:], T.half[:, 0], T.half[:, 1], add).then_inc(S.fin, 1)
        g.sync.wait_ge(S.fin, 1)
        g.sync.dma_start(T.y[:], T.out[:]).then_inc(S.st, 16)
        g.wait_ge(S.st, 16)
    g.wait_ge(S.sent, sent)
